import numpy as np, ml_dtypes
CORES = [35,38,43,46]
N = 4
GR, GC, TK = 2, 2, 128
RA = [[1,2],[-1,-1]]
CB = [[1,-1],[2,-2]]
def setup_inputs(rng):
    return {"x": rng.standard_normal((N, 128, TK), dtype=np.float32).astype(ml_dtypes.bfloat16), "a": (rng.standard_normal((N, 128, 128), dtype=np.float32) / 11).astype(ml_dtypes.bfloat16)}
def setup_inputs_big(rng):
    d = setup_inputs(rng)
    for k in ("x", "a"): d[k] = (d[k].astype(np.float32) * 1024.0).astype(d[k].dtype)
    return d
def setup_inputs_small(rng):
    d = setup_inputs(rng)
    for k in ("x", "a"): d[k] = (d[k].astype(np.float32) * (1 / 1024.0)).astype(d[k].dtype)
    return d
def setup_inputs_apart(rng):
    d = setup_inputs(rng)
    f = (10.0 ** rng.permutation(np.linspace(-1.5, 1.5, N))).astype(np.float32).reshape(N, 1, 1)
    for k in ("x", "a"): d[k] = (d[k].astype(np.float32) * f).astype(d[k].dtype)
    return d
def reference(x, a):
    X, A = x.astype(np.float64), a.astype(np.float64)
    y = np.zeros((N, 128, TK))
    for i in range(GR):
        for j in range(GC):
            t = sum(RA[i][k] * CB[j][l] * X[k * GC + l] for k in range(GR) for l in range(GC))
            y[i * GC + j] = A[i * GC + j].T @ t
    return {"y": y.astype(ml_dtypes.bfloat16)}

from concourse.bass import DstId, RemoteDMATransfer
from concourse.mybir import AluOpType

ENGINES = 4
MAXW = 4

SCRATCH = {
    "xs": ("sbuf", [128, 128], "bfloat16"),
    "a0": ("sbuf", [128, 128], "bfloat16"),
    "ys": ("sbuf", [128, 128], "bfloat16"),
    "acc": ("psum", [128, 128], "float32"),
}
for _r in range(4):
    SCRATCH["land%d" % _r] = ("sbuf", [128, 128], "bfloat16")
for _v in range(MAXW):
    SCRATCH["k%d" % _v] = ("sbuf", [128, 128], "bfloat16")
    SCRATCH["s%d" % _v] = ("sbuf", [128, 128], "bfloat16")

SEMAPHORES = (["xl", "al", "sent", "fill", "mm", "cp", "st"]
              + ["arr%d" % _r for _r in range(4)] + ["sc%d" % _v for _v in range(MAXW)])


def _bits(m):
    return [b for b in range(m.bit_length()) if (m >> b) & 1]


def _weight(T, dst_rank, src_rank):
    ra, cb = T.tables["RA"], T.tables["CB"]
    gc = len(cb)
    return ra[dst_rank // gc][src_rank // gc] * cb[dst_rank % gc][src_rank % gc]


def _plan(T, topo, src):
    sr = T.rank_of(src)
    peers = [d for d in T.cores if d != src and _weight(T, T.rank_of(d), sr) != 0]
    peers.sort(key=lambda d: len(_bits(topo.mask(src, d))))
    narrow = min([len(_bits(topo.mask(src, d))) for d in peers] + [16])
    used, out = 0, []
    for d in peers:
        if not topo.may_write(src, d):
            raise ValueError("core %d may not write to core %d" % (src, d))
        free = [b for b in _bits(topo.mask(src, d)) if not (used >> b) & 1]
        take = free[:ENGINES] if len(_bits(topo.mask(src, d))) == narrow else free[-ENGINES:]
        m = sum(1 << b for b in take)
        used |= m
        out.append((d, m))
    return out


def rank_program(g, core, T, topo):
    rank = T.rank_of(core)
    if rank is None:
        return
    sem = T.sem

    g.sync.dma_start(T.xs[:], T.x[:]).then_inc(sem.xl, 16)
    g.scalar.dma_start(T.a0[:], T.a[:]).then_inc(sem.al, 16)

    mine = _plan(T, topo, core)
    if mine:
        transfers = []
        for d, m in mine:
            rid, pid, _ = topo.addr(d)
            transfers.append(RemoteDMATransfer(dst_ids=[DstId(rid=rid, pnc=pid)], dma_engine_mask=m,
                                               remote_sem=sem["arr%d" % rank],
                                               src=T.xs[:], dst=T["land%d" % rank][:]))
        g.wait_ge(sem.xl, 16)
        g.remote_dma_fused(transfers, local_sem=sem.sent)
        g.wait_ge(sem.sent, sum(len(_bits(m)) for _, m in mine))

    def distance(s):
        return (s != core, topo.chip(s) != topo.chip(core), topo.die(s) != topo.die(core))
    terms = [s for s in sorted(T.cores, key=distance) if _weight(T, rank, T.rank_of(s)) != 0]
    weights = []
    for s in terms:
        w = _weight(T, rank, T.rank_of(s))
        if w != 1 and w not in weights:
            weights.append(w)

    for v, w in enumerate(weights):
        g.vector.memset(T["k%d" % v][:], float(w)).then_inc(sem.fill, 1)
    if weights:
        g.vector.wait_ge(sem.fill, len(weights))
        g.vector.wait_ge(sem.al, 16)
    for v, w in enumerate(weights):
        g.vector.tensor_tensor(T["s%d" % v][:], T.a0[:], T["k%d" % v][:], AluOpType.mult).then_inc(sem["sc%d" % v], 1)

    for n, s in enumerate(terms):
        w = _weight(T, rank, T.rank_of(s))
        if w == 1:
            g.tensor.wait_ge(sem.al, 16)
            lhs = T.a0
        else:
            v = weights.index(w)
            g.tensor.wait_ge(sem["sc%d" % v], 1)
            lhs = T["s%d" % v]
        if s == core:
            g.tensor.wait_ge(sem.xl, 16)
            rhs = T.xs
        else:
            g.tensor.wait_ge(sem["arr%d" % T.rank_of(s)], len(_bits(dict(_plan(T, topo, s))[core])))
            rhs = T["land%d" % T.rank_of(s)]
        g.tensor.matmul(T.acc[:], lhs[:], rhs[:], n == 0, n == len(terms) - 1).then_inc(sem.mm, 1)

    g.vector.wait_ge(sem.mm, len(terms))
    g.vector.tensor_copy(T.ys[:], T.acc[:]).then_inc(sem.cp, 1)
    g.sync.wait_ge(sem.cp, 1)
    g.sync.dma_start(T.y[:], T.ys[:]).then_inc(sem.st, 16)
    g.sync.wait_ge(sem.st, 16)
